import numpy as np
import ml_dtypes


def mxq(x, axis, fmt="e4m3"):
    dtype, down = {"e4m3": (ml_dtypes.float8_e4m3fn, 7), "e5m2": (ml_dtypes.float8_e5m2, 14)}[fmt]
    v = np.moveaxis(np.asarray(x, np.float32).astype(ml_dtypes.bfloat16).astype(np.float64), axis, -1)
    blocks = v.reshape(v.shape[:-1] + (-1, 32))
    amax = np.abs(blocks).max(-1, keepdims=True)
    byte = np.maximum(np.where(amax > 0, np.frexp(amax)[1] - 1 + 127, 0) - down, 1)
    scale = np.exp2(byte - 127.0)
    codes = (blocks / scale).astype(np.float32).astype(dtype).astype(np.float64)
    return np.moveaxis((codes * scale).reshape(v.shape), -1, axis)


WIDE = False


def mx_kscale(k):
    if not WIDE:
        return np.ones(k)
    levels = np.array([10, -10, 5, -5, 0])
    if k % 512:
        return np.exp2(np.random.permutation(np.resize(levels, k // 32))).repeat(32)
    a = np.empty((k // 512, 16))
    for p in range(k // 512):
        a[p, :8] = np.random.permutation(np.resize(levels, 8))
        for g in range(8):
            far = levels[np.abs(levels - a[p, g]) >= 10]
            a[p, g + 8] = far[np.random.randint(len(far))]
    return np.exp2(a.ravel()).repeat(32)


def f64(x):
    return np.asarray(x).astype(np.float64)


def striped(idx):
    return np.tile(idx.reshape(-1, 16).T, (8, 1)).astype(np.uint16)


def unstriped(offs):
    return offs[:16].T.reshape(-1).astype(np.int64)


def striped8(idx):
    return np.concatenate([x.reshape(-1, 16).T for x in idx]).astype(np.uint16)


def runs(offs, k):
    lists = np.stack([offs[16 * r : 16 * r + 16].T.reshape(-1) for r in range(8)]).astype(np.int64)
    return lists[np.arange(k) % 512 // 64]


def pack_weight(w):
    k, n = w.shape
    w = f64(np.asarray(w, np.float32).astype(ml_dtypes.bfloat16)).reshape(k // 32, 32, n)
    amax = np.abs(w).max(1)
    byte = np.clip(np.where(amax > 0, np.frexp(amax)[1] - 1 + 127 - 7, 1), 1, 254)
    scaled = (w * np.exp2(127.0 - byte)[:, None, :]).reshape(k, n).astype(np.float32)
    words = np.ascontiguousarray(scaled.reshape(k // 512, 128, 4, n).transpose(0, 1, 3, 2)).astype(ml_dtypes.float8_e4m3fn).view(np.uint8)
    return words, np.ascontiguousarray(byte.astype(np.uint8).reshape(k // 512, 16, n))


def unpack_weight(words, scales):
    g, p, n, _ = words.shape
    vals = np.ascontiguousarray(words).view(ml_dtypes.float8_e4m3fn).astype(np.float64) * np.repeat(np.exp2(scales.astype(np.float64) - 127.0), 8, axis=1)[..., None]
    return vals.transpose(0, 1, 3, 2).reshape(g * 512, n)


E2M1 = np.array([0.0, 0.5, 1.0, 1.5, 2.0, 3.0, 4.0, 6.0, -0.0, -0.5, -1.0, -1.5, -2.0, -3.0, -4.0, -6.0])


def pack_fp4(w):
    k, n = w.shape
    w = f64(np.asarray(w, np.float32).astype(ml_dtypes.bfloat16)).reshape(k // 32, 32, n)
    amax = np.abs(w).max(1)
    mant, ex = np.frexp(amax / 6.0)
    byte = np.clip(np.where(amax > 0, np.where(mant > 0.5, ex, ex - 1) + 127, 1), 1, 254)
    scaled = (w * np.exp2(127.0 - byte)[:, None, :]).reshape(k, n).astype(np.float32)
    c = np.ascontiguousarray(scaled.reshape(k // 512, 128, 4, n).transpose(0, 1, 3, 2)).astype(ml_dtypes.float4_e2m1fn).view(np.uint8) & 0xF
    words = (c[..., 0::2] | (c[..., 1::2] << 4)).reshape(k // 512, 128, 2 * n)
    return np.ascontiguousarray(words), np.ascontiguousarray(byte.astype(np.uint8).reshape(k // 512, 16, n))


def unpack_fp4(words, scales):
    g, _, n = scales.shape
    words = np.ascontiguousarray(words).reshape(g, 128, n, 2)
    nib = np.empty((g, 128, n, 4), np.uint8)
    nib[..., 0::2] = words & 0xF
    nib[..., 1::2] = words >> 4
    vals = E2M1[nib] * np.repeat(np.exp2(scales.astype(np.float64) - 127.0), 8, axis=1)[..., None]
    return vals.transpose(0, 1, 3, 2).reshape(g * 512, n)


def sigmoid(v):
    return 1.0 / (1.0 + np.exp(-np.maximum(v, -700.0)))

def planes(y):
    n, m = y.shape
    v = y.astype(np.float32).astype(ml_dtypes.bfloat16).astype(np.float64).reshape(n // 32, 32, m)
    top = np.abs(v).max(1)
    byte = np.clip(np.where(top > 0, np.frexp(top)[1] - 1 + 127 - 7, 1), 1, 254)
    codes = (v * np.exp2(127.0 - byte)[:, None, :]).reshape(n, m).astype(np.float32).astype(ml_dtypes.float8_e4m3fn).view(np.uint8)
    words = codes.reshape(n // 512, 128, 4, m).transpose(0, 1, 3, 2)
    return np.ascontiguousarray(words), np.ascontiguousarray(byte.astype(np.uint8).reshape(n // 512, 16, m))


K, T, S, N, H, G, W = 512, 2048, 512, 512, 512, 2048, 256


def setup_inputs():
    n = np.random.standard_normal
    s = mx_kscale(K)[:, None]
    u = mx_kscale(S)
    packed_xT = pack_weight(n((K, T)) * s)
    packed_w1 = pack_fp4(n((K, H)) / np.sqrt(K) / s)
    packed_dT = pack_weight(n((K, G)) / s)
    packed_w2 = pack_fp4(n((H, N)) / np.sqrt(H) / u[:, None])
    perm = np.stack([np.random.permutation(S) for _ in range(8)])
    return {
        "x_words": packed_xT[0],
        "x_scales": packed_xT[1],
        "w1_words": packed_w1[0],
        "w1_scales": packed_w1[1],
        "d_words": packed_dT[0],
        "d_scales": packed_dT[1],
        "gn": (np.random.uniform(0.5, 1.5, (H, 1)) * u[:, None]).astype(np.float32),
        "w2_words": packed_w2[0],
        "w2_scales": packed_w2[1],
        "offs": striped(np.random.permutation(T)[:S]),
        "k1": striped8(np.random.randint(0, G, (8, H))),
        "two": striped(np.random.permutation(T)[:S]),
        "n1": striped(np.random.permutation(S)),
        "n2": striped(np.random.permutation(S)),
        "n3": striped8(perm[:, :W]),
        "n4": striped8(perm[:, W:]),
    }


def reference(x_words, x_scales, w1_words, w1_scales, d_words, d_scales, gn, w2_words, w2_scales, offs, k1, two, n1, n2, n3, n4):
    xq = unpack_weight(x_words, x_scales)[:, unstriped(offs)]
    y = unpack_fp4(w1_words, w1_scales).T @ xq
    d_k1 = unpack_weight(d_words, d_scales)[np.arange(K)[:, None], runs(k1, K)]
    x_two = unpack_weight(x_words, x_scales)[:, unstriped(two)]
    d = 0.0625 * (d_k1.T @ x_two)
    z = f64(gn) * (y[:, unstriped(n1)] - (np.tanh(d) * d[:, unstriped(n2)]))
    h = unpack_fp4(w2_words, w2_scales).T @ mxq(z, 0, "e4m3")
    pb = h[np.arange(N)[:, None], runs(n4, N)]
    pa = h[np.arange(N)[:, None], runs(n3, N)]
    rb = pb * sigmoid(pb - pa)
    ra = pa * sigmoid(pa - pb)
    ds = np.zeros((N, S))
    ds[np.arange(N)[:, None], runs(n3, N)] = ra
    out = ds.copy()
    out[np.arange(N)[:, None], runs(n4, N)] = rb
    return (out,) + planes(out)

@@ -1,0 +1,262 @@
+from contextlib import ExitStack
+
+import concourse.mybir as mybir
+
+F32 = mybir.dt.float32
+BF16 = mybir.dt.bfloat16
+I32 = mybir.dt.int32
+U32 = mybir.dt.uint32
+U16 = mybir.dt.uint16
+U8 = mybir.dt.uint8
+FP8X4 = mybir.dt.float8_e4m3fn_x4
+FP4X4 = mybir.dt.float4_e2m1fn_x4
+ACT = mybir.ActivationFunctionType
+ALU = mybir.AluOpType
+
+P = 128
+SLOTS = 4
+S = 512
+T = 2048
+HALF = 256
+FLOPS = 3 * 2 * 512 * 512 * 512
+
+
+def tile_picked_twkeysoftbduel_none_po_kernel(
+    tc, x_words, x_scales, w1_words, w1_scales, d_words, d_scales, gn, w2_words, w2_scales,
+    offs, k1, two, n1, n2, n3, n4, out_0, out_1, out_2,
+):
+    nc = tc.nc
+    with ExitStack() as ctx:
+        lists = ctx.enter_context(tc.tile_pool(name="lists", bufs=1))
+        sb = ctx.enter_context(tc.tile_pool(name="sb", bufs=1))
+        ps = ctx.enter_context(tc.psum_pool(name="ps", bufs=1))
+
+        def tile(name, shape, dtype, tag=None):
+            return sb.tile(shape, dtype, name=name, tag=tag or name, align_bytes=64)
+
+        def load_list(name, src):
+            held = lists.tile(list(src.shape), U16, name=name)
+            nc.sync.dma_start(held[:], src)
+            return held
+
+        def load_words(name, src, tag=None):
+            held = tile(name, [P, T], I32, tag=tag)
+            nc.sync.dma_start(held[:], src[0].rearrange("p n t -> p (n t)").bitcast(I32))
+            return held
+
+        def load_plane(held, src, queue):
+            for q in range(4):
+                queue.dma_start(held[32 * q : 32 * q + 4, :].bitcast(I32), src[0, 4 * q : 4 * q + 4, :].bitcast(I32))
+
+        def deal(engine, dst, src, run):
+            engine.tensor_copy(
+                dst.rearrange("p (t c i) -> p c t i", t=SLOTS, i=run),
+                src.rearrange("p (c i t) -> p c t i", t=SLOTS, i=run),
+            )
+
+        d_plane = tile("d_plane", [P, T], U8)
+        x_plane = tile("x_plane", [P, T], U8, tag="then_dw")
+        w1_plane = tile("w1_plane", [P, S], U8)
+        dk_plane = tile("dk_plane", [P, S], U8)
+        for plane in (x_plane, w1_plane, d_plane, dk_plane):
+            nc.gpsimd.memset(plane[:].bitcast(I32), 0)
+
+        offs_l = load_list("offs_l", offs)
+        load_plane(x_plane, x_scales, nc.sync)
+        two_l = load_list("two_l", two)
+        xw = load_words("xw", x_words)
+        w1_raw = tile("w1_raw", [P, 2 * S], U8)
+        nc.sync.dma_start(w1_raw[:].bitcast(I32), w1_words[0].bitcast(I32))
+        load_plane(w1_plane, w1_scales, nc.sync)
+        gain = tile("gain", [P, SLOTS], F32)
+        nc.sync.dma_start(gain[:], gn.rearrange("(p t) o -> p (t o)", t=SLOTS))
+        k1_l = load_list("k1_l", k1)
+        for r in range(2):
+            nc.sync.dma_start(d_plane[r:P:16, :].bitcast(I32), d_scales[0, r:16:2, :].bitcast(I32))
+        n1_l = load_list("n1_l", n1)
+
+        gain_d = tile("gain_d", [P, SLOTS], F32)
+        nc.scalar.activation(gain_d[:], gain[:], ACT.Copy, scale=-0.0625)
+
+        def deal_fp4(name, raw, plane, tags=(None, None)):
+            words = tile(name + "_words", [P, 2 * S], U8, tag=tags[0])
+            deal(nc.vector, words[:].bitcast(U16), raw[:].bitcast(U16), 8)
+            scales = tile(name + "_scales", [P, S], U8, tag=tags[1])
+            deal(nc.vector, scales[:], plane[:], 16)
+            return words, scales
+
+        xo_s = tile("xo_s", [P, S], U8)
+        nc.vector.tensor_copy(xo_s[:], x_plane[:].indirect(offs_l[:]))
+        xt_s = tile("xt_s", [P, S], U8)
+        nc.vector.tensor_copy(xt_s[:], x_plane[:].indirect(two_l[:]))
+        dw = load_words("dw", d_words, tag="then_dw")
+        n2_l = load_list("n2_l", n2)
+        xo_w = tile("xo_w", [P, S], U32)
+        nc.vector.tensor_copy(xo_w[:], xw[:].bitcast(U32).indirect(offs_l[:]))
+        w1w, w1s = deal_fp4("w1", w1_raw, w1_plane)
+        y_ps = [ps.tile([P, S], F32, name=f"y_ps{t}", tag=f"b{t}") for t in range(SLOTS)]
+        for t in range(SLOTS):
+            nc.tensor.matmul_mx(
+                out=y_ps[t][:], lhsT=w1w[:, 2 * t * P : 2 * (t + 1) * P].bitcast(FP4X4),
+                lhsT_scale=w1s[:, t * P : (t + 1) * P],
+                rhs=xo_w[:].bitcast(FP8X4), rhs_scale=xo_s[:], start=True, stop=True,
+            )
+
+        dk_bytes = tile("dk_bytes", [P, S], U8, tag="then_xt_w")
+        nc.vector.tensor_copy(dk_bytes[:], d_plane[:].indirect(k1_l[:]))
+        dk_dealt = tile("dk_dealt", [P, S], U8)
+        deal(nc.vector, dk_dealt[:], dk_bytes[:], 16)
+        for r in range(4):
+            src = 16 * (r // 2) + r % 2
+            nc.sync.dma_start(dk_plane[r:P:32, :].bitcast(I32), dk_dealt[src:P:32, :].bitcast(I32))
+
+        nc.sync.dma_start(w1_raw[:].bitcast(I32), w2_words[0].bitcast(I32))
+        load_plane(w1_plane, w2_scales, nc.sync)
+        n3_l = load_list("n3_l", n3)
+        n4_l = load_list("n4_l", n4)
+        xt_w = tile("xt_w", [P, S], U32, tag="then_xt_w")
+        nc.vector.tensor_copy(xt_w[:], xw[:].bitcast(U32).indirect(two_l[:]))
+        dk_w = tile("dk_w", [P, S], U32)
+        nc.vector.tensor_copy(dk_w[:], dw[:].bitcast(U32).indirect(k1_l[:]))
+        dk_wd = tile("dk_wd", [P, S], U32, tag="then_picked")
+        deal(nc.vector, dk_wd[:], dk_w[:], 4)
+
+        d_ps = [ps.tile([P, S], F32, name=f"d_ps{t}", tag=f"a{t}") for t in range(SLOTS)]
+        for t in range(SLOTS):
+            cols = slice(t * P, (t + 1) * P)
+            nc.tensor.matmul_mx(
+                out=d_ps[t][:], lhsT=dk_wd[:, cols].bitcast(FP8X4), lhsT_scale=dk_plane[:, cols],
+                rhs=xt_w[:].bitcast(FP8X4), rhs_scale=xt_s[:], start=True, stop=True,
+            )
+
+        halves = [slice(0, HALF), slice(HALF, S)]
+        list_halves = [slice(0, HALF // 16), slice(HALF // 16, S // 16)]
+
+        gy = [tile(f"gy{t}", [P, S], F32) for t in range(SLOTS)]
+        picked = [tile("picked0", [P, SLOTS, HALF], F32), None]
+        for t in range(SLOTS):
+            nc.scalar.activation(gy[t][:], y_ps[t][:], ACT.Copy, scale=gain[:, t : t + 1])
+            nc.scalar.activation(picked[0][:, t, :], gy[t][:].indirect(n1_l[:, list_halves[0]]), ACT.Copy)
+
+        tanh_d = tile("tanh_d", [P, SLOTS, S], F32)
+        prod = [tile(f"prod{u}", [P, SLOTS, HALF], F32) for u in range(2)]
+        gd = [tile(f"gd{t}", [P, S], F32) for t in range(SLOTS)]
+        nc.vector.tensor_scalar(gd[1][:], d_ps[1][:], gain_d[:, 1:2], None, ALU.mult)
+        w2w, w2s = deal_fp4("w2", w1_raw, w1_plane, ("dk_w", "dk_dealt"))
+        for t in range(SLOTS):
+            cols = halves[0] if t == SLOTS - 1 else slice(0, S)
+            nc.scalar.activation(tanh_d[:, t, cols], d_ps[t][:, cols], ACT.Tanh, scale=0.0625)
+            if t != 1:
+                nc.scalar.activation(gd[t][:], d_ps[t][:], ACT.Copy, scale=gain_d[:, t : t + 1])
+
+        def times_tanh(t, u):
+            nc.vector.tensor_tensor(
+                prod[u][:, t, :], gd[t][:].indirect(n2_l[:, list_halves[u]]), tanh_d[:, t, halves[u]], ALU.mult
+            )
+
+        picked[1] = tile("picked1", [P, SLOTS, HALF], F32, tag="then_picked")
+        for t in range(SLOTS):
+            nc.scalar.activation(picked[1][:, t, :], gy[t][:].indirect(n1_l[:, list_halves[1]]), ACT.Copy)
+            if t == 1:
+                nc.scalar.activation(tanh_d[:, 3, halves[1]], d_ps[3][:, halves[1]], ACT.Tanh, scale=0.0625)
+
+        zb = [tile(f"zb{u}", [P, HALF * SLOTS], BF16) for u in range(2)]
+        hh = [tile(f"hh{t}", [P, S], F32, tag=f"h_then_fb{t}") for t in range(SLOTS)]
+        h_ps = {}
+
+        def add_round(u):
+            nc.vector.tensor_tensor(
+                zb[u][:].rearrange("p (c i t) -> p c t i", t=SLOTS, i=4),
+                picked[u][:].rearrange("p t (c i) -> p c t i", i=4),
+                prod[u][:].rearrange("p t (c i) -> p c t i", i=4),
+                ALU.add,
+            )
+
+        def second_product(u):
+            zw = tile(f"zw{u}", [P, HALF], U32)
+            zs = tile(f"zs{u}", [P, HALF], U8)
+            nc.vector.quantize_mx(out=zw[:].bitcast(FP8X4), scales=zs[:], in_=zb[u][:])
+            for t in range(SLOTS):
+                h_ps[t, u] = ps.tile([P, HALF], F32, name=f"h_ps{t}_{u}", tag=f"{'ba'[u]}{t}")
+                nc.tensor.matmul_mx(
+                    out=h_ps[t, u][:], lhsT=w2w[:, 2 * t * P : 2 * (t + 1) * P].bitcast(FP4X4),
+                    lhsT_scale=w2s[:, t * P : (t + 1) * P],
+                    rhs=zw[:].bitcast(FP8X4), rhs_scale=zs[:], start=True, stop=True,
+                )
+
+        def leave_bank(t, u):
+            nc.scalar.activation(hh[t][:, halves[u]], h_ps[t, u][:], ACT.Copy)
+
+        for t in range(SLOTS - 1):
+            times_tanh(t, 0)
+            times_tanh(t, 1)
+        times_tanh(SLOTS - 1, 0)
+        add_round(0)
+        times_tanh(SLOTS - 1, 1)
+        second_product(0)
+        add_round(1)
+        second_product(1)
+        for t in range(SLOTS):
+            leave_bank(t, 0)
+
+        out_rows = out_0.rearrange("(p t) c -> p t c", t=SLOTS)
+        res = [tile(f"res{t}", [P, S], F32) for t in range(SLOTS)]
+        pair, gap, fa = {}, {}, {}
+
+        def fetch(t):
+            leave_bank(t, 1)
+            pair[t] = tile(f"pair{t}", [P, 2, HALF], F32, tag=f"gap_then_pair{t - 1}")
+            nc.scalar.activation(pair[t][:, 0, :], hh[t][:].indirect(n3_l[:]), ACT.Copy)
+            if t == 0:
+                nc.vector.tensor_copy(pair[t][:, 1, :], hh[t][:].indirect(n4_l[:]))
+            else:
+                nc.scalar.activation(pair[t][:, 1, :], hh[t][:].indirect(n4_l[:]), ACT.Copy)
+            gap[t] = tile(f"gap{t}", [P, HALF], F32, tag=f"gap_then_pair{t}")
+            nc.vector.tensor_tensor(gap[t][:], pair[t][:, 0, :], pair[t][:, 1, :], ALU.subtract)
+
+        def put_a(t):
+            fa[t] = tile(f"fa{t}", [P, HALF], F32)
+            nc.scalar.activation(fa[t][:], gap[t][:], ACT.Sigmoid)
+            nc.vector.tensor_tensor(res[t][:].indirect(n3_l[:]), pair[t][:, 0, :], fa[t][:], ALU.mult)
+
+        def put_b(t):
+            fb = tile(f"fb{t}", [P, HALF], F32, tag=f"h_then_fb{t + 1}")
+            nc.scalar.activation(fb[:], fa[t][:], ACT.Copy, scale=-1.0, bias=1.0)
+            nc.vector.tensor_tensor(res[t][:].indirect(n4_l[:]), pair[t][:, 1, :], fb[:], ALU.mult)
+            nc.sync.dma_start(out_rows[:, t, :], res[t][:])
+
+        def round_out(t, u):
+            if u == 0 and t >= 2:
+                nc.vector.tensor_copy(ob[u][:, :, t], res[t][:, halves[u]])
+            else:
+                nc.scalar.copy(ob[u][:, :, t], res[t][:, halves[u]])
+
+        fetch(0)
+        for t in range(SLOTS - 1):
+            put_a(t)
+            fetch(t + 1)
+            put_b(t)
+        put_a(3)
+        rounded = tile("rounded", [P, S, SLOTS], BF16, tag="gap_then_pair3")
+        ob = [rounded[:, halves[u], :] for u in range(2)]
+        round_out(2, 0)
+        put_b(3)
+        for t in range(2):
+            round_out(t, 0)
+            round_out(t, 1)
+        round_out(2, 1)
+        round_out(3, 1)
+        round_out(3, 0)
+
+        ow = tile("ow", [P, S], U32)
+        osc = tile("osc", [P, S], U8)
+        words_out = out_1[0].rearrange("p n t -> p (n t)").bitcast(I32)
+        for u in range(2):
+            nc.vector.quantize_mx(
+                out=ow[:, halves[u]].bitcast(FP8X4), scales=osc[:, halves[u]],
+                in_=ob[u].rearrange("p c t -> p (c t)"),
+            )
+            nc.sync.dma_start(words_out[:, halves[u]], ow[:, halves[u]].bitcast(I32))
+        for q in range(4):
+            queue = nc.scalar if q % 2 else nc.sync
+            queue.dma_start(out_2[0, 4 * q : 4 * q + 4, :].bitcast(I32), osc[32 * q : 32 * q + 4, :].bitcast(I32))

@@ -44,9 +44,9 @@ def tile_picked_twkeysoftbduel_none_po_kernel(
             nc.sync.dma_start(held[:], src[0].rearrange("p n t -> p (n t)").bitcast(I32))
             return held
 
-        def load_plane(held, src, queue):
+        def load_plane(held, src, *queues):
             for q in range(4):
-                queue.dma_start(held[32 * q : 32 * q + 4, :].bitcast(I32), src[0, 4 * q : 4 * q + 4, :].bitcast(I32))
+                queues[q % len(queues)].dma_start(held[32 * q : 32 * q + 4, :].bitcast(I32), src[0, 4 * q : 4 * q + 4, :].bitcast(I32))
 
         def deal(engine, dst, src, run):
             engine.tensor_copy(
@@ -55,45 +55,59 @@ def tile_picked_twkeysoftbduel_none_po_kernel(
             )
 
         d_plane = tile("d_plane", [P, T], U8)
-        x_plane = tile("x_plane", [P, T], U8, tag="then_dw")
+        x_plane = tile("x_plane", [P, T], U8)
         w1_plane = tile("w1_plane", [P, S], U8)
-        dk_plane = tile("dk_plane", [P, S], U8)
-        for plane in (x_plane, w1_plane, d_plane, dk_plane):
-            nc.gpsimd.memset(plane[:].bitcast(I32), 0)
+        w2_plane = tile("w2_plane", [P, S], U8)
+        nc.gpsimd.memset(x_plane[:].bitcast(I32), 0)
+        for plane in (d_plane, w1_plane, w2_plane):
+            nc.vector.memset(plane[:].bitcast(I32), 0)
+        warm = tile("warm", [P, 2], F32)
+        nc.vector.memset(warm[:, 0:1], 0.0)
 
         offs_l = load_list("offs_l", offs)
-        load_plane(x_plane, x_scales, nc.sync)
+        load_plane(x_plane, x_scales, nc.sync, nc.scalar)
         two_l = load_list("two_l", two)
         xw = load_words("xw", x_words)
         w1_raw = tile("w1_raw", [P, 2 * S], U8)
         nc.sync.dma_start(w1_raw[:].bitcast(I32), w1_words[0].bitcast(I32))
         load_plane(w1_plane, w1_scales, nc.sync)
-        gain = tile("gain", [P, SLOTS], F32)
-        nc.sync.dma_start(gain[:], gn.rearrange("(p t) o -> p (t o)", t=SLOTS))
         k1_l = load_list("k1_l", k1)
+        gain = tile("gain", [P, SLOTS], F32)
+        w2_raw = tile("w2_raw", [P, 2 * S], U8)
+        nc.sync.dma_start(w2_raw[:].bitcast(I32), w2_words[0].bitcast(I32))
         for r in range(2):
-            nc.sync.dma_start(d_plane[r:P:16, :].bitcast(I32), d_scales[0, r:16:2, :].bitcast(I32))
+            nc.gpsimd.dma_start(d_plane[r:P:16, :].bitcast(I32), d_scales[0, r:16:2, :].bitcast(I32))
+        nc.gpsimd.dma_start(gain[:], gn.rearrange("(p t) o -> p (t o)", t=SLOTS))
         n1_l = load_list("n1_l", n1)
+        dw = load_words("dw", d_words)
+        load_plane(w2_plane, w2_scales, nc.sync)
 
+        nc.scalar.activation(warm[:, 1:2], warm[:, 0:1], ACT.Sigmoid)
         gain_d = tile("gain_d", [P, SLOTS], F32)
         nc.scalar.activation(gain_d[:], gain[:], ACT.Copy, scale=-0.0625)
 
-        def deal_fp4(name, raw, plane, tags=(None, None)):
-            words = tile(name + "_words", [P, 2 * S], U8, tag=tags[0])
-            deal(nc.vector, words[:].bitcast(U16), raw[:].bitcast(U16), 8)
-            scales = tile(name + "_scales", [P, S], U8, tag=tags[1])
-            deal(nc.vector, scales[:], plane[:], 16)
-            return words, scales
+        def deal_fp4_words(name, raw, tag=None):
+            words = tile(name, [P, 2 * S], U8, tag=tag)
+            nc.scalar.copy(
+                words[:].bitcast(U16).rearrange("p (t c i) -> p c t i", t=SLOTS, i=8),
+                raw[:].bitcast(U16).rearrange("p (c i t) -> p c t i", t=SLOTS, i=8),
+            )
+            return words
+
+        def deal_scales(name, plane, engine, tag=None):
+            scales = tile(name, [P, S], U8, tag=tag)
+            deal(engine, scales[:], plane[:], 16)
+            return scales
 
         xo_s = tile("xo_s", [P, S], U8)
         nc.vector.tensor_copy(xo_s[:], x_plane[:].indirect(offs_l[:]))
         xt_s = tile("xt_s", [P, S], U8)
         nc.vector.tensor_copy(xt_s[:], x_plane[:].indirect(two_l[:]))
-        dw = load_words("dw", d_words, tag="then_dw")
-        n2_l = load_list("n2_l", n2)
         xo_w = tile("xo_w", [P, S], U32)
         nc.vector.tensor_copy(xo_w[:], xw[:].bitcast(U32).indirect(offs_l[:]))
-        w1w, w1s = deal_fp4("w1", w1_raw, w1_plane)
+        w1w = deal_fp4_words("w1w", w1_raw)
+        w2w = deal_fp4_words("w2w", w2_raw)
+        w1s = deal_scales("w1s", w1_plane, nc.gpsimd)
         y_ps = [ps.tile([P, S], F32, name=f"y_ps{t}", tag=f"b{t}") for t in range(SLOTS)]
         for t in range(SLOTS):
             nc.tensor.matmul_mx(
@@ -104,16 +118,14 @@ def tile_picked_twkeysoftbduel_none_po_kernel(
 
         dk_bytes = tile("dk_bytes", [P, S], U8, tag="then_xt_w")
         nc.vector.tensor_copy(dk_bytes[:], d_plane[:].indirect(k1_l[:]))
-        dk_dealt = tile("dk_dealt", [P, S], U8)
-        deal(nc.vector, dk_dealt[:], dk_bytes[:], 16)
-        for r in range(4):
-            src = 16 * (r // 2) + r % 2
-            nc.sync.dma_start(dk_plane[r:P:32, :].bitcast(I32), dk_dealt[src:P:32, :].bitcast(I32))
-
-        nc.sync.dma_start(w1_raw[:].bitcast(I32), w2_words[0].bitcast(I32))
-        load_plane(w1_plane, w2_scales, nc.sync)
+        dk_plane = tile("dk_plane", [P, S], U8)
+        deal(nc.vector, dk_plane[:], dk_bytes[:], 16)
+        for r in range(2):
+            nc.sync.dma_start(dk_plane[2 + r : P : 32, :].bitcast(I32), dk_plane[16 + r : P : 32, :].bitcast(I32))
+        n2_l = load_list("n2_l", n2)
         n3_l = load_list("n3_l", n3)
         n4_l = load_list("n4_l", n4)
+
         xt_w = tile("xt_w", [P, S], U32, tag="then_xt_w")
         nc.vector.tensor_copy(xt_w[:], xw[:].bitcast(U32).indirect(two_l[:]))
         dk_w = tile("dk_w", [P, S], U32)
@@ -121,8 +133,10 @@ def tile_picked_twkeysoftbduel_none_po_kernel(
         dk_wd = tile("dk_wd", [P, S], U32, tag="then_picked")
         deal(nc.vector, dk_wd[:], dk_w[:], 4)
 
-        d_ps = [ps.tile([P, S], F32, name=f"d_ps{t}", tag=f"a{t}") for t in range(SLOTS)]
-        for t in range(SLOTS):
+        d_ps = {}
+
+        def d_product(t):
+            d_ps[t] = ps.tile([P, S], F32, name=f"d_ps{t}", tag=f"a{t % 2}")
             cols = slice(t * P, (t + 1) * P)
             nc.tensor.matmul_mx(
                 out=d_ps[t][:], lhsT=dk_wd[:, cols].bitcast(FP8X4), lhsT_scale=dk_plane[:, cols],
@@ -141,12 +155,14 @@ def tile_picked_twkeysoftbduel_none_po_kernel(
         tanh_d = tile("tanh_d", [P, SLOTS, S], F32)
         prod = [tile(f"prod{u}", [P, SLOTS, HALF], F32) for u in range(2)]
         gd = [tile(f"gd{t}", [P, S], F32) for t in range(SLOTS)]
-        nc.vector.tensor_scalar(gd[1][:], d_ps[1][:], gain_d[:, 1:2], None, ALU.mult)
-        w2w, w2s = deal_fp4("w2", w1_raw, w1_plane, ("dk_w", "dk_dealt"))
+        w2s = deal_scales("w2s", w2_plane, nc.vector, "dk_w")
         for t in range(SLOTS):
+            d_product(t)
+            if t < 2:
+                nc.vector.tensor_scalar(gd[t][:], d_ps[t][:], gain_d[:, t : t + 1], None, ALU.mult)
             cols = halves[0] if t == SLOTS - 1 else slice(0, S)
             nc.scalar.activation(tanh_d[:, t, cols], d_ps[t][:, cols], ACT.Tanh, scale=0.0625)
-            if t != 1:
+            if t >= 2:
                 nc.scalar.activation(gd[t][:], d_ps[t][:], ACT.Copy, scale=gain_d[:, t : t + 1])
 
         def times_tanh(t, u):
@@ -159,9 +175,11 @@ def tile_picked_twkeysoftbduel_none_po_kernel(
             nc.scalar.activation(picked[1][:, t, :], gy[t][:].indirect(n1_l[:, list_halves[1]]), ACT.Copy)
             if t == 1:
                 nc.scalar.activation(tanh_d[:, 3, halves[1]], d_ps[3][:, halves[1]], ACT.Tanh, scale=0.0625)
+                last_d = tile("last_d", [P, HALF], F32)
+                nc.scalar.activation(last_d[:], gd[3][:].indirect(n2_l[:, list_halves[1]]), ACT.Copy)
 
         zb = [tile(f"zb{u}", [P, HALF * SLOTS], BF16) for u in range(2)]
-        hh = [tile(f"hh{t}", [P, S], F32, tag=f"h_then_fb{t}") for t in range(SLOTS)]
+        hh = {}
         h_ps = {}
 
         def add_round(u):
@@ -172,17 +190,20 @@ def tile_picked_twkeysoftbduel_none_po_kernel(
                 ALU.add,
             )
 
-        def second_product(u):
-            zw = tile(f"zw{u}", [P, HALF], U32)
-            zs = tile(f"zs{u}", [P, HALF], U8)
-            nc.vector.quantize_mx(out=zw[:].bitcast(FP8X4), scales=zs[:], in_=zb[u][:])
-            for t in range(SLOTS):
-                h_ps[t, u] = ps.tile([P, HALF], F32, name=f"h_ps{t}_{u}", tag=f"{'ba'[u]}{t}")
-                nc.tensor.matmul_mx(
-                    out=h_ps[t, u][:], lhsT=w2w[:, 2 * t * P : 2 * (t + 1) * P].bitcast(FP4X4),
-                    lhsT_scale=w2s[:, t * P : (t + 1) * P],
-                    rhs=zw[:].bitcast(FP8X4), rhs_scale=zs[:], start=True, stop=True,
-                )
+        zw, zs = {}, {}
+
+        def quantise_z(u):
+            zw[u] = tile(f"zw{u}", [P, HALF], U32)
+            zs[u] = tile(f"zs{u}", [P, HALF], U8)
+            nc.vector.quantize_mx(out=zw[u][:].bitcast(FP8X4), scales=zs[u][:], in_=zb[u][:])
+
+        def h_product(t, u):
+            h_ps[t, u] = ps.tile([P, HALF], F32, name=f"h_ps{t}_{u}", tag="a0" if u else f"b{t}")
+            nc.tensor.matmul_mx(
+                out=h_ps[t, u][:], lhsT=w2w[:, 2 * t * P : 2 * (t + 1) * P].bitcast(FP4X4),
+                lhsT_scale=w2s[:, t * P : (t + 1) * P],
+                rhs=zw[u][:].bitcast(FP8X4), rhs_scale=zs[u][:], start=True, stop=True,
+            )
 
         def leave_bank(t, u):
             nc.scalar.activation(hh[t][:, halves[u]], h_ps[t, u][:], ACT.Copy)
@@ -192,18 +213,25 @@ def tile_picked_twkeysoftbduel_none_po_kernel(
             times_tanh(t, 1)
         times_tanh(SLOTS - 1, 0)
         add_round(0)
-        times_tanh(SLOTS - 1, 1)
-        second_product(0)
+        nc.vector.tensor_tensor(prod[1][:, 3, :], last_d[:], tanh_d[:, 3, halves[1]], ALU.mult)
+        quantise_z(0)
         add_round(1)
-        second_product(1)
+        quantise_z(1)
         for t in range(SLOTS):
-            leave_bank(t, 0)
+            h_product(t, 0)
+            if t < 2:
+                hh[t] = tile(f"hh{t}", [P, S], F32, tag=f"h_then_fb{t}")
+                leave_bank(t, 0)
 
         out_rows = out_0.rearrange("(p t) c -> p t c", t=SLOTS)
         res = [tile(f"res{t}", [P, S], F32) for t in range(SLOTS)]
         pair, gap, fa = {}, {}, {}
 
         def fetch(t):
+            if t >= 2:
+                hh[t] = tile(f"hh{t}", [P, S], F32, tag=f"h_then_fb{t}")
+                leave_bank(t, 0)
+            h_product(t, 1)
             leave_bank(t, 1)
             pair[t] = tile(f"pair{t}", [P, 2, HALF], F32, tag=f"gap_then_pair{t - 1}")
             nc.scalar.activation(pair[t][:, 0, :], hh[t][:].indirect(n3_l[:]), ACT.Copy)
@@ -215,7 +243,7 @@ def tile_picked_twkeysoftbduel_none_po_kernel(
             nc.vector.tensor_tensor(gap[t][:], pair[t][:, 0, :], pair[t][:, 1, :], ALU.subtract)
 
         def put_a(t):
-            fa[t] = tile(f"fa{t}", [P, HALF], F32)
+            fa[t] = tile(f"fa{t}", [P, HALF], F32, tag=f"h_then_fb{t + 2}" if t < 2 else None)
             nc.scalar.activation(fa[t][:], gap[t][:], ACT.Sigmoid)
             nc.vector.tensor_tensor(res[t][:].indirect(n3_l[:]), pair[t][:, 0, :], fa[t][:], ALU.mult)
 

@@ -57,30 +57,27 @@ def tile_picked_twkeysoftbduel_none_po_kernel(
         d_plane = tile("d_plane", [P, T], U8)
         x_plane = tile("x_plane", [P, T], U8)
         w1_plane = tile("w1_plane", [P, S], U8)
-        w2_plane = tile("w2_plane", [P, S], U8)
-        nc.gpsimd.memset(x_plane[:].bitcast(I32), 0)
-        for plane in (d_plane, w1_plane, w2_plane):
+        for plane in (x_plane, d_plane, w1_plane):
             nc.vector.memset(plane[:].bitcast(I32), 0)
         warm = tile("warm", [P, 2], F32)
         nc.vector.memset(warm[:, 0:1], 0.0)
 
+        gain = tile("gain", [P, SLOTS], F32)
+        nc.gpsimd.dma_start(gain[:], gn.rearrange("(p t) o -> p (t o)", t=SLOTS))
+        w2_raw = tile("w2_raw", [P, 2 * S], U8)
+        nc.gpsimd.dma_start(w2_raw[:].bitcast(I32), w2_words[0].bitcast(I32))
         offs_l = load_list("offs_l", offs)
+        k1_l = load_list("k1_l", k1)
         load_plane(x_plane, x_scales, nc.sync, nc.scalar)
-        two_l = load_list("two_l", two)
+        for r, queue in enumerate((nc.sync, nc.scalar)):
+            queue.dma_start(d_plane[r:P:16, :].bitcast(I32), d_scales[0, r:16:2, :].bitcast(I32))
         xw = load_words("xw", x_words)
         w1_raw = tile("w1_raw", [P, 2 * S], U8)
         nc.sync.dma_start(w1_raw[:].bitcast(I32), w1_words[0].bitcast(I32))
         load_plane(w1_plane, w1_scales, nc.sync)
-        k1_l = load_list("k1_l", k1)
-        gain = tile("gain", [P, SLOTS], F32)
-        w2_raw = tile("w2_raw", [P, 2 * S], U8)
-        nc.sync.dma_start(w2_raw[:].bitcast(I32), w2_words[0].bitcast(I32))
-        for r in range(2):
-            nc.gpsimd.dma_start(d_plane[r:P:16, :].bitcast(I32), d_scales[0, r:16:2, :].bitcast(I32))
-        nc.gpsimd.dma_start(gain[:], gn.rearrange("(p t) o -> p (t o)", t=SLOTS))
-        n1_l = load_list("n1_l", n1)
+        two_l = load_list("two_l", two)
         dw = load_words("dw", d_words)
-        load_plane(w2_plane, w2_scales, nc.sync)
+        n1_l = load_list("n1_l", n1)
 
         nc.scalar.activation(warm[:, 1:2], warm[:, 0:1], ACT.Sigmoid)
         gain_d = tile("gain_d", [P, SLOTS], F32)
@@ -101,22 +98,7 @@ def tile_picked_twkeysoftbduel_none_po_kernel(
 
         xo_s = tile("xo_s", [P, S], U8)
         nc.vector.tensor_copy(xo_s[:], x_plane[:].indirect(offs_l[:]))
-        xt_s = tile("xt_s", [P, S], U8)
-        nc.vector.tensor_copy(xt_s[:], x_plane[:].indirect(two_l[:]))
-        xo_w = tile("xo_w", [P, S], U32)
-        nc.vector.tensor_copy(xo_w[:], xw[:].bitcast(U32).indirect(offs_l[:]))
-        w1w = deal_fp4_words("w1w", w1_raw)
-        w2w = deal_fp4_words("w2w", w2_raw)
-        w1s = deal_scales("w1s", w1_plane, nc.gpsimd)
-        y_ps = [ps.tile([P, S], F32, name=f"y_ps{t}", tag=f"b{t}") for t in range(SLOTS)]
-        for t in range(SLOTS):
-            nc.tensor.matmul_mx(
-                out=y_ps[t][:], lhsT=w1w[:, 2 * t * P : 2 * (t + 1) * P].bitcast(FP4X4),
-                lhsT_scale=w1s[:, t * P : (t + 1) * P],
-                rhs=xo_w[:].bitcast(FP8X4), rhs_scale=xo_s[:], start=True, stop=True,
-            )
-
-        dk_bytes = tile("dk_bytes", [P, S], U8, tag="then_xt_w")
+        dk_bytes = tile("dk_bytes", [P, S], U8)
         nc.vector.tensor_copy(dk_bytes[:], d_plane[:].indirect(k1_l[:]))
         dk_plane = tile("dk_plane", [P, S], U8)
         deal(nc.vector, dk_plane[:], dk_bytes[:], 16)
@@ -126,7 +108,23 @@ def tile_picked_twkeysoftbduel_none_po_kernel(
         n3_l = load_list("n3_l", n3)
         n4_l = load_list("n4_l", n4)
 
-        xt_w = tile("xt_w", [P, S], U32, tag="then_xt_w")
+        xo_w = tile("xo_w", [P, S], U32)
+        nc.vector.tensor_copy(xo_w[:], xw[:].bitcast(U32).indirect(offs_l[:]))
+        w1w = deal_fp4_words("w1w", w1_raw)
+        w2w = deal_fp4_words("w2w", w2_raw)
+        w1s = deal_scales("w1s", w1_plane, nc.vector)
+        load_plane(w1_plane, w2_scales, nc.sync, nc.scalar)
+        y_ps = [ps.tile([P, S], F32, name=f"y_ps{t}", tag=f"b{t}") for t in range(SLOTS)]
+        for t in range(SLOTS):
+            nc.tensor.matmul_mx(
+                out=y_ps[t][:], lhsT=w1w[:, 2 * t * P : 2 * (t + 1) * P].bitcast(FP4X4),
+                lhsT_scale=w1s[:, t * P : (t + 1) * P],
+                rhs=xo_w[:].bitcast(FP8X4), rhs_scale=xo_s[:], start=True, stop=True,
+            )
+
+        xt_s = tile("xt_s", [P, S], U8)
+        nc.vector.tensor_copy(xt_s[:], x_plane[:].indirect(two_l[:]))
+        xt_w = tile("xt_w", [P, S], U32)
         nc.vector.tensor_copy(xt_w[:], xw[:].bitcast(U32).indirect(two_l[:]))
         dk_w = tile("dk_w", [P, S], U32)
         nc.vector.tensor_copy(dk_w[:], dw[:].bitcast(U32).indirect(k1_l[:]))
@@ -146,16 +144,19 @@ def tile_picked_twkeysoftbduel_none_po_kernel(
         halves = [slice(0, HALF), slice(HALF, S)]
         list_halves = [slice(0, HALF // 16), slice(HALF // 16, S // 16)]
 
-        gy = [tile(f"gy{t}", [P, S], F32) for t in range(SLOTS)]
+        gy = [tile(f"gy{t}", [P, S], F32, tag="dk_w" if t == SLOTS - 1 else None) for t in range(SLOTS)]
         picked = [tile("picked0", [P, SLOTS, HALF], F32), None]
         for t in range(SLOTS):
-            nc.scalar.activation(gy[t][:], y_ps[t][:], ACT.Copy, scale=gain[:, t : t + 1])
+            if t < SLOTS - 1:
+                nc.scalar.activation(gy[t][:], y_ps[t][:], ACT.Copy, scale=gain[:, t : t + 1])
+            else:
+                nc.vector.tensor_scalar(gy[t][:], y_ps[t][:], gain[:, t : t + 1], None, ALU.mult)
             nc.scalar.activation(picked[0][:, t, :], gy[t][:].indirect(n1_l[:, list_halves[0]]), ACT.Copy)
 
         tanh_d = tile("tanh_d", [P, SLOTS, S], F32)
         prod = [tile(f"prod{u}", [P, SLOTS, HALF], F32) for u in range(2)]
         gd = [tile(f"gd{t}", [P, S], F32) for t in range(SLOTS)]
-        w2s = deal_scales("w2s", w2_plane, nc.vector, "dk_w")
+        w2s = deal_scales("w2s", w1_plane, nc.vector)
         for t in range(SLOTS):
             d_product(t)
             if t < 2:

@@ -179,74 +179,86 @@ def tile_picked_twkeysoftbduel_none_po_kernel(
                 last_d = tile("last_d", [P, HALF], F32)
                 nc.scalar.activation(last_d[:], gd[3][:].indirect(n2_l[:, list_halves[1]]), ACT.Copy)
 
-        zb = [tile(f"zb{u}", [P, HALF * SLOTS], BF16) for u in range(2)]
+        zb = [tile(f"zb{u}", [P, HALF, SLOTS], BF16) for u in range(2)]
         hh = {}
-        h_ps = {}
 
-        def add_round(u):
+        zw = tile("zw", [P, S], U32)
+        zs = tile("zs", [P, S], U8)
+
+        def add_round(u, part):
             nc.vector.tensor_tensor(
-                zb[u][:].rearrange("p (c i t) -> p c t i", t=SLOTS, i=4),
-                picked[u][:].rearrange("p t (c i) -> p c t i", i=4),
-                prod[u][:].rearrange("p t (c i) -> p c t i", i=4),
+                zb[u][:, part, :].rearrange("p (c i) t -> p c t i", i=4),
+                picked[u][:, :, part].rearrange("p t (c i) -> p c t i", i=4),
+                prod[u][:, :, part].rearrange("p t (c i) -> p c t i", i=4),
                 ALU.add,
             )
 
-        zw, zs = {}, {}
-
-        def quantise_z(u):
-            zw[u] = tile(f"zw{u}", [P, HALF], U32)
-            zs[u] = tile(f"zs{u}", [P, HALF], U8)
-            nc.vector.quantize_mx(out=zw[u][:].bitcast(FP8X4), scales=zs[u][:], in_=zb[u][:])
-
-        def h_product(t, u):
-            h_ps[t, u] = ps.tile([P, HALF], F32, name=f"h_ps{t}_{u}", tag="a0" if u else f"b{t}")
-            nc.tensor.matmul_mx(
-                out=h_ps[t, u][:], lhsT=w2w[:, 2 * t * P : 2 * (t + 1) * P].bitcast(FP4X4),
-                lhsT_scale=w2s[:, t * P : (t + 1) * P],
-                rhs=zw[u][:].bitcast(FP8X4), rhs_scale=zs[u][:], start=True, stop=True,
+        def quantise_z(u, part):
+            cols = slice(u * HALF + part.start, u * HALF + part.stop)
+            nc.vector.quantize_mx(
+                out=zw[:, cols].bitcast(FP8X4), scales=zs[:, cols], in_=zb[u][:, part, :].rearrange("p c t -> p (c t)")
             )
 
-        def leave_bank(t, u):
-            nc.scalar.activation(hh[t][:, halves[u]], h_ps[t, u][:], ACT.Copy)
+        def h_columns(t, cols, bank):
+            acc = ps.tile([P, cols.stop - cols.start], F32, name=f"h_ps{t}_{cols.start}", tag=bank)
+            nc.tensor.matmul_mx(
+                out=acc[:], lhsT=w2w[:, 2 * t * P : 2 * (t + 1) * P].bitcast(FP4X4),
+                lhsT_scale=w2s[:, t * P : (t + 1) * P],
+                rhs=zw[:, cols].bitcast(FP8X4), rhs_scale=zs[:, cols], start=True, stop=True,
+            )
+            nc.scalar.activation(hh[t][:, cols], acc[:], ACT.Copy)
 
         for t in range(SLOTS - 1):
             times_tanh(t, 0)
             times_tanh(t, 1)
         times_tanh(SLOTS - 1, 0)
-        add_round(0)
+        add_round(0, slice(0, HALF))
         nc.vector.tensor_tensor(prod[1][:, 3, :], last_d[:], tanh_d[:, 3, halves[1]], ALU.mult)
-        quantise_z(0)
-        add_round(1)
-        quantise_z(1)
-        for t in range(SLOTS):
-            h_product(t, 0)
-            if t < 2:
-                hh[t] = tile(f"hh{t}", [P, S], F32, tag=f"h_then_fb{t}")
-                leave_bank(t, 0)
+        quantise_z(0, slice(0, HALF))
+        quarters = [slice(0, P), slice(P, HALF)]
+        for part in quarters:
+            add_round(1, part)
+        for part in quarters:
+            quantise_z(1, part)
+        for t in range(2):
+            hh[t] = tile(f"hh{t}", [P, S], F32, tag=f"h_then_fb{t}")
+            h_columns(t, halves[0], f"b{t}")
 
         out_rows = out_0.rearrange("(p t) c -> p t c", t=SLOTS)
         res = [tile(f"res{t}", [P, S], F32) for t in range(SLOTS)]
         pair, gap, fa = {}, {}, {}
 
+        def pieces(t):
+            width = HALF // 2 if t == 0 else HALF
+            return [(slice(c, c + width), slice(c // 16, (c + width) // 16)) for c in range(0, HALF, width)]
+
         def fetch(t):
-            if t >= 2:
-                hh[t] = tile(f"hh{t}", [P, S], F32, tag=f"h_then_fb{t}")
-                leave_bank(t, 0)
-            h_product(t, 1)
-            leave_bank(t, 1)
-            pair[t] = tile(f"pair{t}", [P, 2, HALF], F32, tag=f"gap_then_pair{t - 1}")
-            nc.scalar.activation(pair[t][:, 0, :], hh[t][:].indirect(n3_l[:]), ACT.Copy)
             if t == 0:
-                nc.vector.tensor_copy(pair[t][:, 1, :], hh[t][:].indirect(n4_l[:]))
+                h_columns(t, slice(HALF, HALF + P), "a1")
+                h_columns(t, slice(HALF + P, S), "a0")
+            elif t == 1:
+                h_columns(t, halves[1], "a0")
             else:
-                nc.scalar.activation(pair[t][:, 1, :], hh[t][:].indirect(n4_l[:]), ACT.Copy)
+                hh[t] = tile(f"hh{t}", [P, S], F32, tag=f"h_then_fb{t}")
+                h_columns(t, slice(0, S), "a0")
+            pair[t] = tile(f"pair{t}", [P, 2, HALF], F32, tag=f"gap_then_pair{t - 1}")
             gap[t] = tile(f"gap{t}", [P, HALF], F32, tag=f"gap_then_pair{t}")
-            nc.vector.tensor_tensor(gap[t][:], pair[t][:, 0, :], pair[t][:, 1, :], ALU.subtract)
+            for cols, entries in pieces(t):
+                nc.scalar.activation(pair[t][:, 0, cols], hh[t][:].indirect(n3_l[:, entries]), ACT.Copy)
+                if t == 0:
+                    nc.vector.tensor_copy(pair[t][:, 1, cols], hh[t][:].indirect(n4_l[:, entries]))
+                else:
+                    nc.scalar.activation(pair[t][:, 1, cols], hh[t][:].indirect(n4_l[:, entries]), ACT.Copy)
+            for cols, entries in pieces(t):
+                nc.vector.tensor_tensor(gap[t][:, cols], pair[t][:, 0, cols], pair[t][:, 1, cols], ALU.subtract)
 
         def put_a(t):
             fa[t] = tile(f"fa{t}", [P, HALF], F32, tag=f"h_then_fb{t + 2}" if t < 2 else None)
-            nc.scalar.activation(fa[t][:], gap[t][:], ACT.Sigmoid)
-            nc.vector.tensor_tensor(res[t][:].indirect(n3_l[:]), pair[t][:, 0, :], fa[t][:], ALU.mult)
+            for cols, entries in pieces(t):
+                nc.scalar.activation(fa[t][:, cols], gap[t][:, cols], ACT.Sigmoid)
+                nc.vector.tensor_tensor(
+                    res[t][:].indirect(n3_l[:, entries]), pair[t][:, 0, cols], fa[t][:, cols], ALU.mult
+                )
 
         def put_b(t):
             fb = tile(f"fb{t}", [P, HALF], F32, tag=f"h_then_fb{t + 1}")

from contextlib import ExitStack

import concourse.mybir as mybir

F32 = mybir.dt.float32
BF16 = mybir.dt.bfloat16
I32 = mybir.dt.int32
U32 = mybir.dt.uint32
U16 = mybir.dt.uint16
U8 = mybir.dt.uint8
FP8X4 = mybir.dt.float8_e4m3fn_x4
FP4X4 = mybir.dt.float4_e2m1fn_x4
ACT = mybir.ActivationFunctionType
ALU = mybir.AluOpType

P = 128
SLOTS = 4
S = 512
T = 2048
HALF = 256
FLOPS = 3 * 2 * 512 * 512 * 512


def tile_picked_twkeysoftbduel_none_po_kernel(
    tc, x_words, x_scales, w1_words, w1_scales, d_words, d_scales, gn, w2_words, w2_scales,
    offs, k1, two, n1, n2, n3, n4, out_0, out_1, out_2,
):
    nc = tc.nc
    with ExitStack() as ctx:
        lists = ctx.enter_context(tc.tile_pool(name="lists", bufs=1))
        sb = ctx.enter_context(tc.tile_pool(name="sb", bufs=1))
        ps = ctx.enter_context(tc.psum_pool(name="ps", bufs=1))

        def tile(name, shape, dtype, tag=None):
            return sb.tile(shape, dtype, name=name, tag=tag or name, align_bytes=64)

        def load_list(name, src):
            held = lists.tile(list(src.shape), U16, name=name)
            nc.sync.dma_start(held[:], src)
            return held

        def load_words(name, src, tag=None):
            held = tile(name, [P, T], I32, tag=tag)
            nc.sync.dma_start(held[:], src[0].rearrange("p n t -> p (n t)").bitcast(I32))
            return held

        def load_plane(held, src, *queues):
            for q in range(4):
                queues[q % len(queues)].dma_start(held[32 * q : 32 * q + 4, :].bitcast(I32), src[0, 4 * q : 4 * q + 4, :].bitcast(I32))

        def deal(engine, dst, src, run):
            engine.tensor_copy(
                dst.rearrange("p (t c i) -> p c t i", t=SLOTS, i=run),
                src.rearrange("p (c i t) -> p c t i", t=SLOTS, i=run),
            )

        d_plane = tile("d_plane", [P, T], U8)
        x_plane = tile("x_plane", [P, T], U8)
        w1_plane = tile("w1_plane", [P, S], U8)
        for plane in (x_plane, d_plane, w1_plane):
            nc.vector.memset(plane[:].bitcast(I32), 0)
        warm = tile("warm", [P, 2], F32)
        nc.vector.memset(warm[:, 0:1], 0.0)

        gain = tile("gain", [P, SLOTS], F32)
        nc.gpsimd.dma_start(gain[:], gn.rearrange("(p t) o -> p (t o)", t=SLOTS))
        w2_raw = tile("w2_raw", [P, 2 * S], U8)
        nc.gpsimd.dma_start(w2_raw[:].bitcast(I32), w2_words[0].bitcast(I32))
        offs_l = load_list("offs_l", offs)
        k1_l = load_list("k1_l", k1)
        load_plane(x_plane, x_scales, nc.sync, nc.scalar)
        for r, queue in enumerate((nc.sync, nc.scalar)):
            queue.dma_start(d_plane[r:P:16, :].bitcast(I32), d_scales[0, r:16:2, :].bitcast(I32))
        xw = load_words("xw", x_words)
        w1_raw = tile("w1_raw", [P, 2 * S], U8)
        nc.sync.dma_start(w1_raw[:].bitcast(I32), w1_words[0].bitcast(I32))
        load_plane(w1_plane, w1_scales, nc.sync)
        two_l = load_list("two_l", two)
        dw = load_words("dw", d_words)
        n1_l = load_list("n1_l", n1)

        nc.scalar.activation(warm[:, 1:2], warm[:, 0:1], ACT.Sigmoid)
        gain_d = tile("gain_d", [P, SLOTS], F32)
        nc.scalar.activation(gain_d[:], gain[:], ACT.Copy, scale=-0.0625)

        def deal_fp4_words(name, raw, tag=None):
            words = tile(name, [P, 2 * S], U8, tag=tag)
            nc.scalar.copy(
                words[:].bitcast(U16).rearrange("p (t c i) -> p c t i", t=SLOTS, i=8),
                raw[:].bitcast(U16).rearrange("p (c i t) -> p c t i", t=SLOTS, i=8),
            )
            return words

        def deal_scales(name, plane, engine, tag=None):
            scales = tile(name, [P, S], U8, tag=tag)
            deal(engine, scales[:], plane[:], 16)
            return scales

        xo_s = tile("xo_s", [P, S], U8)
        nc.vector.tensor_copy(xo_s[:], x_plane[:].indirect(offs_l[:]))
        dk_bytes = tile("dk_bytes", [P, S], U8)
        nc.vector.tensor_copy(dk_bytes[:], d_plane[:].indirect(k1_l[:]))
        dk_plane = tile("dk_plane", [P, S], U8)
        deal(nc.vector, dk_plane[:], dk_bytes[:], 16)
        for r in range(2):
            nc.sync.dma_start(dk_plane[2 + r : P : 32, :].bitcast(I32), dk_plane[16 + r : P : 32, :].bitcast(I32))
        n2_l = load_list("n2_l", n2)
        n3_l = load_list("n3_l", n3)
        n4_l = load_list("n4_l", n4)

        xo_w = tile("xo_w", [P, S], U32)
        nc.vector.tensor_copy(xo_w[:], xw[:].bitcast(U32).indirect(offs_l[:]))
        w1w = deal_fp4_words("w1w", w1_raw)
        w2w = deal_fp4_words("w2w", w2_raw)
        w1s = deal_scales("w1s", w1_plane, nc.vector)
        load_plane(w1_plane, w2_scales, nc.sync, nc.scalar)
        y_ps = [ps.tile([P, S], F32, name=f"y_ps{t}", tag=f"b{t}") for t in range(SLOTS)]
        for t in range(SLOTS):
            nc.tensor.matmul_mx(
                out=y_ps[t][:], lhsT=w1w[:, 2 * t * P : 2 * (t + 1) * P].bitcast(FP4X4),
                lhsT_scale=w1s[:, t * P : (t + 1) * P],
                rhs=xo_w[:].bitcast(FP8X4), rhs_scale=xo_s[:], start=True, stop=True,
            )

        xt_s = tile("xt_s", [P, S], U8)
        nc.vector.tensor_copy(xt_s[:], x_plane[:].indirect(two_l[:]))
        xt_w = tile("xt_w", [P, S], U32)
        nc.vector.tensor_copy(xt_w[:], xw[:].bitcast(U32).indirect(two_l[:]))
        dk_w = tile("dk_w", [P, S], U32)
        nc.vector.tensor_copy(dk_w[:], dw[:].bitcast(U32).indirect(k1_l[:]))
        dk_wd = tile("dk_wd", [P, S], U32, tag="then_picked")
        deal(nc.vector, dk_wd[:], dk_w[:], 4)

        d_ps = {}

        def d_product(t):
            d_ps[t] = ps.tile([P, S], F32, name=f"d_ps{t}", tag=f"a{t % 2}")
            cols = slice(t * P, (t + 1) * P)
            nc.tensor.matmul_mx(
                out=d_ps[t][:], lhsT=dk_wd[:, cols].bitcast(FP8X4), lhsT_scale=dk_plane[:, cols],
                rhs=xt_w[:].bitcast(FP8X4), rhs_scale=xt_s[:], start=True, stop=True,
            )

        halves = [slice(0, HALF), slice(HALF, S)]
        list_halves = [slice(0, HALF // 16), slice(HALF // 16, S // 16)]

        gy = [tile(f"gy{t}", [P, S], F32, tag="dk_w" if t == SLOTS - 1 else None) for t in range(SLOTS)]
        picked = [tile("picked0", [P, SLOTS, HALF], F32), None]
        for t in range(SLOTS):
            if t < SLOTS - 1:
                nc.scalar.activation(gy[t][:], y_ps[t][:], ACT.Copy, scale=gain[:, t : t + 1])
            else:
                nc.vector.tensor_scalar(gy[t][:], y_ps[t][:], gain[:, t : t + 1], None, ALU.mult)
            nc.scalar.activation(picked[0][:, t, :], gy[t][:].indirect(n1_l[:, list_halves[0]]), ACT.Copy)

        tanh_d = tile("tanh_d", [P, SLOTS, S], F32)
        prod = [tile(f"prod{u}", [P, SLOTS, HALF], F32) for u in range(2)]
        gd = [tile(f"gd{t}", [P, S], F32) for t in range(SLOTS)]
        w2s = deal_scales("w2s", w1_plane, nc.vector)
        for t in range(SLOTS):
            d_product(t)
            if t < 2:
                nc.vector.tensor_scalar(gd[t][:], d_ps[t][:], gain_d[:, t : t + 1], None, ALU.mult)
            cols = halves[0] if t == SLOTS - 1 else slice(0, S)
            nc.scalar.activation(tanh_d[:, t, cols], d_ps[t][:, cols], ACT.Tanh, scale=0.0625)
            if t >= 2:
                nc.scalar.activation(gd[t][:], d_ps[t][:], ACT.Copy, scale=gain_d[:, t : t + 1])

        def times_tanh(t, u):
            nc.vector.tensor_tensor(
                prod[u][:, t, :], gd[t][:].indirect(n2_l[:, list_halves[u]]), tanh_d[:, t, halves[u]], ALU.mult
            )

        picked[1] = tile("picked1", [P, SLOTS, HALF], F32, tag="then_picked")
        for t in range(SLOTS):
            nc.scalar.activation(picked[1][:, t, :], gy[t][:].indirect(n1_l[:, list_halves[1]]), ACT.Copy)
            if t == 1:
                nc.scalar.activation(tanh_d[:, 3, halves[1]], d_ps[3][:, halves[1]], ACT.Tanh, scale=0.0625)
                last_d = tile("last_d", [P, HALF], F32)
                nc.scalar.activation(last_d[:], gd[3][:].indirect(n2_l[:, list_halves[1]]), ACT.Copy)

        zb = [tile(f"zb{u}", [P, HALF, SLOTS], BF16) for u in range(2)]
        hh = {}

        zw = tile("zw", [P, S], U32)
        zs = tile("zs", [P, S], U8)

        def add_round(u, part):
            nc.vector.tensor_tensor(
                zb[u][:, part, :].rearrange("p (c i) t -> p c t i", i=4),
                picked[u][:, :, part].rearrange("p t (c i) -> p c t i", i=4),
                prod[u][:, :, part].rearrange("p t (c i) -> p c t i", i=4),
                ALU.add,
            )

        def quantise_z(u, part):
            cols = slice(u * HALF + part.start, u * HALF + part.stop)
            nc.vector.quantize_mx(
                out=zw[:, cols].bitcast(FP8X4), scales=zs[:, cols], in_=zb[u][:, part, :].rearrange("p c t -> p (c t)")
            )

        def h_columns(t, cols, bank):
            acc = ps.tile([P, cols.stop - cols.start], F32, name=f"h_ps{t}_{cols.start}", tag=bank)
            nc.tensor.matmul_mx(
                out=acc[:], lhsT=w2w[:, 2 * t * P : 2 * (t + 1) * P].bitcast(FP4X4),
                lhsT_scale=w2s[:, t * P : (t + 1) * P],
                rhs=zw[:, cols].bitcast(FP8X4), rhs_scale=zs[:, cols], start=True, stop=True,
            )
            nc.scalar.activation(hh[t][:, cols], acc[:], ACT.Copy)

        for t in range(SLOTS - 1):
            times_tanh(t, 0)
            times_tanh(t, 1)
        times_tanh(SLOTS - 1, 0)
        add_round(0, slice(0, HALF))
        nc.vector.tensor_tensor(prod[1][:, 3, :], last_d[:], tanh_d[:, 3, halves[1]], ALU.mult)
        quantise_z(0, slice(0, HALF))
        quarters = [slice(0, P), slice(P, HALF)]
        for part in quarters:
            add_round(1, part)
        for part in quarters:
            quantise_z(1, part)
        for t in range(2):
            hh[t] = tile(f"hh{t}", [P, S], F32, tag=f"h_then_fb{t}")
            h_columns(t, halves[0], f"b{t}")

        out_rows = out_0.rearrange("(p t) c -> p t c", t=SLOTS)
        res = [tile(f"res{t}", [P, S], F32) for t in range(SLOTS)]
        pair, gap, fa = {}, {}, {}

        def pieces(t):
            width = HALF // 2 if t == 0 else HALF
            return [(slice(c, c + width), slice(c // 16, (c + width) // 16)) for c in range(0, HALF, width)]

        def fetch(t):
            if t == 0:
                h_columns(t, slice(HALF, HALF + P), "a1")
                h_columns(t, slice(HALF + P, S), "a0")
            elif t == 1:
                h_columns(t, halves[1], "a0")
            else:
                hh[t] = tile(f"hh{t}", [P, S], F32, tag=f"h_then_fb{t}")
                h_columns(t, slice(0, S), "a0")
            pair[t] = tile(f"pair{t}", [P, 2, HALF], F32, tag=f"gap_then_pair{t - 1}")
            gap[t] = tile(f"gap{t}", [P, HALF], F32, tag=f"gap_then_pair{t}")
            for cols, entries in pieces(t):
                nc.scalar.activation(pair[t][:, 0, cols], hh[t][:].indirect(n3_l[:, entries]), ACT.Copy)
                if t == 0:
                    nc.vector.tensor_copy(pair[t][:, 1, cols], hh[t][:].indirect(n4_l[:, entries]))
                else:
                    nc.scalar.activation(pair[t][:, 1, cols], hh[t][:].indirect(n4_l[:, entries]), ACT.Copy)
            for cols, entries in pieces(t):
                nc.vector.tensor_tensor(gap[t][:, cols], pair[t][:, 0, cols], pair[t][:, 1, cols], ALU.subtract)

        def put_a(t):
            fa[t] = tile(f"fa{t}", [P, HALF], F32, tag=f"h_then_fb{t + 2}" if t < 2 else None)
            for cols, entries in pieces(t):
                nc.scalar.activation(fa[t][:, cols], gap[t][:, cols], ACT.Sigmoid)
                nc.vector.tensor_tensor(
                    res[t][:].indirect(n3_l[:, entries]), pair[t][:, 0, cols], fa[t][:, cols], ALU.mult
                )

        def put_b(t):
            fb = tile(f"fb{t}", [P, HALF], F32, tag=f"h_then_fb{t + 1}")
            nc.scalar.activation(fb[:], fa[t][:], ACT.Copy, scale=-1.0, bias=1.0)
            nc.vector.tensor_tensor(res[t][:].indirect(n4_l[:]), pair[t][:, 1, :], fb[:], ALU.mult)
            nc.sync.dma_start(out_rows[:, t, :], res[t][:])

        def round_out(t, u):
            if u == 0 and t >= 2:
                nc.vector.tensor_copy(ob[u][:, :, t], res[t][:, halves[u]])
            else:
                nc.scalar.copy(ob[u][:, :, t], res[t][:, halves[u]])

        fetch(0)
        for t in range(SLOTS - 1):
            put_a(t)
            fetch(t + 1)
            put_b(t)
        put_a(3)
        rounded = tile("rounded", [P, S, SLOTS], BF16, tag="gap_then_pair3")
        ob = [rounded[:, halves[u], :] for u in range(2)]
        round_out(2, 0)
        put_b(3)
        for t in range(2):
            round_out(t, 0)
            round_out(t, 1)
        round_out(2, 1)
        round_out(3, 1)
        round_out(3, 0)

        ow = tile("ow", [P, S], U32)
        osc = tile("osc", [P, S], U8)
        words_out = out_1[0].rearrange("p n t -> p (n t)").bitcast(I32)
        for u in range(2):
            nc.vector.quantize_mx(
                out=ow[:, halves[u]].bitcast(FP8X4), scales=osc[:, halves[u]],
                in_=ob[u].rearrange("p c t -> p (c t)"),
            )
            nc.sync.dma_start(words_out[:, halves[u]], ow[:, halves[u]].bitcast(I32))
        for q in range(4):
            queue = nc.scalar if q % 2 else nc.sync
            queue.dma_start(out_2[0, 4 * q : 4 * q + 4, :].bitcast(I32), osc[32 * q : 32 * q + 4, :].bitcast(I32))
